import numpy as np
import ml_dtypes


def mxq(x, axis, fmt="e4m3"):
    dtype, down = {"e4m3": (ml_dtypes.float8_e4m3fn, 7), "e5m2": (ml_dtypes.float8_e5m2, 14)}[fmt]
    v = np.moveaxis(np.asarray(x, np.float32).astype(ml_dtypes.bfloat16).astype(np.float64), axis, -1)
    blocks = v.reshape(v.shape[:-1] + (-1, 32))
    amax = np.abs(blocks).max(-1, keepdims=True)
    byte = np.maximum(np.where(amax > 0, np.frexp(amax)[1] - 1 + 127, 0) - down, 1)
    scale = np.exp2(byte - 127.0)
    codes = (blocks / scale).astype(np.float32).astype(dtype).astype(np.float64)
    return np.moveaxis((codes * scale).reshape(v.shape), -1, axis)


WIDE = False


def mx_kscale(k):
    if not WIDE:
        return np.ones(k)
    levels = np.array([10, -10, 5, -5, 0])
    if k % 512:
        return np.exp2(np.random.permutation(np.resize(levels, k // 32))).repeat(32)
    a = np.empty((k // 512, 16))
    for p in range(k // 512):
        a[p, :8] = np.random.permutation(np.resize(levels, 8))
        for g in range(8):
            far = levels[np.abs(levels - a[p, g]) >= 10]
            a[p, g + 8] = far[np.random.randint(len(far))]
    return np.exp2(a.ravel()).repeat(32)


def f64(x):
    return np.asarray(x).astype(np.float64)


def striped(idx):
    return np.tile(idx.reshape(-1, 16).T, (8, 1)).astype(np.uint16)


def unstriped(offs):
    return offs[:16].T.reshape(-1).astype(np.int64)


def striped8(idx):
    return np.concatenate([x.reshape(-1, 16).T for x in idx]).astype(np.uint16)


def runs(offs, k):
    lists = np.stack([offs[16 * r : 16 * r + 16].T.reshape(-1) for r in range(8)]).astype(np.int64)
    return lists[np.arange(k) % 512 // 64]


def pack_weight(w):
    k, n = w.shape
    w = f64(np.asarray(w, np.float32).astype(ml_dtypes.bfloat16)).reshape(k // 32, 32, n)
    amax = np.abs(w).max(1)
    byte = np.clip(np.where(amax > 0, np.frexp(amax)[1] - 1 + 127 - 7, 1), 1, 254)
    scaled = (w * np.exp2(127.0 - byte)[:, None, :]).reshape(k, n).astype(np.float32)
    words = np.ascontiguousarray(scaled.reshape(k // 512, 128, 4, n).transpose(0, 1, 3, 2)).astype(ml_dtypes.float8_e4m3fn).view(np.uint8)
    return words, np.ascontiguousarray(byte.astype(np.uint8).reshape(k // 512, 16, n))


def unpack_weight(words, scales):
    g, p, n, _ = words.shape
    vals = np.ascontiguousarray(words).view(ml_dtypes.float8_e4m3fn).astype(np.float64) * np.repeat(np.exp2(scales.astype(np.float64) - 127.0), 8, axis=1)[..., None]
    return vals.transpose(0, 1, 3, 2).reshape(g * 512, n)


E2M1 = np.array([0.0, 0.5, 1.0, 1.5, 2.0, 3.0, 4.0, 6.0, -0.0, -0.5, -1.0, -1.5, -2.0, -3.0, -4.0, -6.0])


def pack_fp4(w):
    k, n = w.shape
    w = f64(np.asarray(w, np.float32).astype(ml_dtypes.bfloat16)).reshape(k // 32, 32, n)
    amax = np.abs(w).max(1)
    mant, ex = np.frexp(amax / 6.0)
    byte = np.clip(np.where(amax > 0, np.where(mant > 0.5, ex, ex - 1) + 127, 1), 1, 254)
    scaled = (w * np.exp2(127.0 - byte)[:, None, :]).reshape(k, n).astype(np.float32)
    c = np.ascontiguousarray(scaled.reshape(k // 512, 128, 4, n).transpose(0, 1, 3, 2)).astype(ml_dtypes.float4_e2m1fn).view(np.uint8) & 0xF
    words = (c[..., 0::2] | (c[..., 1::2] << 4)).reshape(k // 512, 128, 2 * n)
    return np.ascontiguousarray(words), np.ascontiguousarray(byte.astype(np.uint8).reshape(k // 512, 16, n))


def unpack_fp4(words, scales):
    g, _, n = scales.shape
    words = np.ascontiguousarray(words).reshape(g, 128, n, 2)
    nib = np.empty((g, 128, n, 4), np.uint8)
    nib[..., 0::2] = words & 0xF
    nib[..., 1::2] = words >> 4
    vals = E2M1[nib] * np.repeat(np.exp2(scales.astype(np.float64) - 127.0), 8, axis=1)[..., None]
    return vals.transpose(0, 1, 3, 2).reshape(g * 512, n)


def planes(y):
    n, m = y.shape
    v = y.astype(np.float32).astype(ml_dtypes.bfloat16).astype(np.float64).reshape(n // 32, 32, m)
    top = np.abs(v).max(1)
    byte = np.clip(np.where(top > 0, np.frexp(top)[1] - 1 + 127 - 7, 1), 1, 254)
    codes = (v * np.exp2(127.0 - byte)[:, None, :]).reshape(n, m).astype(np.float32).astype(ml_dtypes.float8_e4m3fn).view(np.uint8)
    words = codes.reshape(n // 512, 128, 4, m).transpose(0, 1, 3, 2)
    return np.ascontiguousarray(words), np.ascontiguousarray(byte.astype(np.uint8).reshape(n // 512, 16, m))


K, T, S, H, C = 512, 2048, 512, 512, 512


def setup_inputs():
    n = np.random.standard_normal
    s = mx_kscale(K)[:, None]
    packed_xT = pack_weight(n((K, T)) * s)
    packed_w1 = pack_fp4(n((K, H)) / np.sqrt(K) / s)
    return {
        "x_words": packed_xT[0],
        "x_scales": packed_xT[1],
        "w1_words": packed_w1[0],
        "w1_scales": packed_w1[1],
        "gs": (np.random.uniform(0.5, 1.5, (K, 1)) / s).astype(np.float32),
        "offs": striped(np.random.permutation(T)[:S]),
        "n1": striped8(np.stack([np.random.permutation(S) for _ in range(8)])),
        "n2": striped8(np.stack([np.random.permutation(S) for _ in range(8)])),
        "ca": striped(np.random.permutation(T)[:C]),
        "cb": striped(np.random.permutation(T)[:C]),
        "n3": striped8(np.stack([np.random.permutation(S) for _ in range(8)])),
        "n4": striped8(np.stack([np.random.permutation(S) for _ in range(8)])),
    }


def reference(x_words, x_scales, w1_words, w1_scales, gs, offs, n1, n2, ca, cb, n3, n4):
    x_ca = unpack_weight(x_words, x_scales)[:, unstriped(ca)]
    xq = unpack_weight(x_words, x_scales)[:, unstriped(offs)]
    y = unpack_fp4(w1_words, w1_scales).T @ xq
    st = np.maximum(y, y[np.arange(H)[:, None], runs(n1, H)])
    z = f64(gs) * (st[np.arange(H)[:, None], runs(n2, H)] - (0.5 * y))
    zq = mxq(z, 0, "e4m3")
    a = 0.0625 * (x_ca.T @ zq)
    x_cb = unpack_weight(x_words, x_scales)[:, unstriped(cb)]
    b = 0.0625 * (x_cb.T @ zq)
    out_0 = a[np.arange(C)[:, None], runs(n3, C)] - (np.tanh(b) * (b[np.arange(C)[:, None], runs(n4, C)]))
    return (out_0,) + planes(out_0)

@@ -1,0 +1,225 @@
+from contextlib import ExitStack
+
+import concourse.mybir as mybir
+
+K, T, S, H, C = 512, 2048, 512, 512, 512
+FLOPS = 3 * 2 * 512 * 512 * 512
+
+F32 = mybir.dt.float32
+BF16 = mybir.dt.bfloat16
+I32 = mybir.dt.int32
+U32 = mybir.dt.uint32
+U16 = mybir.dt.uint16
+U8 = mybir.dt.uint8
+FP8X4 = mybir.dt.float8_e4m3fn_x4
+FP4X4 = mybir.dt.float4_e2m1fn_x4
+ALU = mybir.AluOpType
+ACT = mybir.ActivationFunctionType
+
+P = 128
+PACK = 4
+PIECES = ((0, 256), (256, 384), (384, 512))
+
+
+def tile_picked_ccmpsoftbhopb_none_po_kernel(tc, x_words, x_scales, w1_words, w1_scales, gs, offs, n1, n2, ca, cb, n3, n4, out_0, out_1, out_2):
+    nc = tc.nc
+    with ExitStack() as ctx:
+        lists = ctx.enter_context(tc.tile_pool(name="lists", bufs=1))
+        sb = ctx.enter_context(tc.tile_pool(name="sb", bufs=1))
+        psum = ctx.enter_context(tc.psum_pool(name="psum", bufs=1))
+
+        def tile(name, shape, dtype, tag=None):
+            return sb.tile(shape, dtype, name=name, tag=tag or name, align_bytes=64)
+
+        def load_list(name, src):
+            dst = lists.tile([P, S // 16], U16, name=name)
+            nc.sync.dma_start(dst[:], src)
+            return dst
+
+        def load_scale_rows(engines, dst, src):
+            for q, engine in enumerate(engines):
+                engine.dma_start(dst[32 * q : 32 * q + 4, :].bitcast(I32), src[0, 4 * q : 4 * q + 4, :].bitcast(I32))
+
+        def deal(dst, src):
+            nc.vector.tensor_copy(dst[:].rearrange("p (t m) -> p m t", t=PACK), src[:].rearrange("p (m t) -> p m t", t=PACK))
+
+        xs = tile("xs", [P, T], U8)
+        nc.vector.memset(xs[:].bitcast(I32), 0)
+        ws_raw = tile("ws_raw", [P, H], U8)
+        nc.vector.memset(ws_raw[:].bitcast(I32), 0)
+
+        offs_t = load_list("offs_t", offs)
+        ww_raw = tile("ww_raw", [P, 2 * H], U8)
+        nc.sync.dma_start(ww_raw[:].bitcast(I32), w1_words[0].bitcast(I32))
+        xw = tile("xw", [P, T], U32)
+        nc.sync.dma_start(xw[:].bitcast(I32), x_words[0].rearrange("p n t -> p (n t)").bitcast(I32))
+        load_scale_rows([nc.sync] * 4, xs, x_scales)
+        load_scale_rows([nc.sync, nc.sync, nc.gpsimd, nc.gpsimd], ws_raw, w1_scales)
+        cb_t = load_list("cb_t", cb)
+        n1_t = load_list("n1_t", n1)
+        n2_t = load_list("n2_t", n2)
+        gs_t = tile("gs_t", [P, PACK], F32)
+        nc.sync.dma_start(gs_t[:], gs.rearrange("(p t) o -> p (t o)", t=PACK))
+        ca_t = load_list("ca_t", ca)
+        n4_t = load_list("n4_t", n4)
+        n3_t = load_list("n3_t", n3)
+
+        half = [tile(f"half{t}", [P, 2 * S], F32) for t in range(PACK)]
+        for t in range(PACK):
+            nc.vector.memset(half[t][:, S:], 0.0)
+
+        warm = tile("warm", [P, 1], F32)
+        nc.scalar.activation(warm[:], half[0][:, S : S + 1], ACT.Tanh)
+
+        ww = tile("ww", [P, 2 * H], U8)
+        nc.vector.tensor_copy(
+            ww[:].rearrange("p (t m b) -> p m t b", t=PACK, b=2),
+            ww_raw[:].rearrange("p (m t b) -> p m t b", t=PACK, b=2),
+        )
+        xq_s = tile("xq_s", [P, S], U8)
+        nc.vector.tensor_copy(xq_s[:], xs[:].indirect(offs_t[:]))
+        xq_w = tile("xq_w", [P, S], U32)
+        nc.vector.tensor_copy(xq_w[:], xw[:].indirect(offs_t[:]))
+        ws = tile("ws", [P, H], U8)
+        deal(ws, ws_raw)
+
+        y_ps = []
+        for t in range(PACK):
+            acc = psum.tile([P, S], F32, name=f"y{t}", tag=f"low{t}")
+            nc.tensor.matmul_mx(
+                acc[:],
+                lhsT=ww[:, 2 * P * t : 2 * P * (t + 1)].bitcast(FP4X4),
+                lhsT_scale=ws[:, P * t : P * (t + 1)],
+                rhs=xq_w[:].bitcast(FP8X4),
+                rhs_scale=xq_s[:],
+                start=True,
+                stop=True,
+            )
+            nc.scalar.activation(half[t][:, :S], acc[:], ACT.Copy, scale=0.5)
+            y_ps.append(acc)
+
+        cb_w_raw = tile("cb_w_raw", [P, C], U32)
+        nc.vector.tensor_copy(cb_w_raw[:], xw[:].indirect(cb_t[:]))
+
+        st = [tile(f"st{t}", [P, 2 * S], F32) for t in range(PACK)]
+        diff = [tile(f"diff{t}", [P, S], F32) for t in range(PACK)]
+        z_bf = tile("z_bf", [P, S, PACK], BF16)
+
+        def fetch_y(t):
+            nc.vector.tensor_copy(st[t][:, S:], half[t][:].indirect(n1_t[:]))
+
+        def larger(t):
+            nc.vector.scalar_tensor_tensor(st[t][:, :S], st[t][:, S:], 2.0, y_ps[t][:], ALU.mult, ALU.max)
+
+        def fetch_st(t):
+            nc.vector.tensor_tensor(diff[t][:], st[t][:].indirect(n2_t[:]), half[t][:, :S], ALU.subtract)
+            nc.scalar.activation(z_bf[:, :, t], diff[t][:], ACT.Copy, scale=gs_t[:, t : t + 1])
+
+        fetch_y(0)
+        fetch_y(1)
+        larger(0)
+        larger(1)
+        fetch_st(0)
+        fetch_y(2)
+        fetch_st(1)
+        larger(2)
+        fetch_y(3)
+        fetch_st(2)
+        larger(3)
+        cb_w = tile("cb_w", [P, C], U32, tag="st2")
+        deal(cb_w, cb_w_raw)
+        fetch_st(3)
+        cb_s_raw = tile("cb_s_raw", [P, C], U8, tag="st3")
+        nc.vector.tensor_copy(cb_s_raw[:], xs[:].indirect(cb_t[:]))
+        cb_s = tile("cb_s", [P, C], U8)
+        deal(cb_s, cb_s_raw)
+
+        z_w = tile("z_w", [P, S], U32)
+        z_s = tile("z_s", [P, S], U8)
+        nc.vector.quantize_mx(z_w[:].bitcast(FP8X4), z_s[:], z_bf[:].rearrange("p c t -> p (c t)"))
+
+        ca_w_raw = tile("ca_w_raw", [P, C], U32, tag="z_bf")
+        nc.vector.tensor_copy(ca_w_raw[:], xw[:].indirect(ca_t[:]))
+        ca_s_raw = tile("ca_s_raw", [P, C], U8, tag="diff3")
+        nc.vector.tensor_copy(ca_s_raw[:], xs[:].indirect(ca_t[:]))
+        ca_w = tile("ca_w", [P, C], U32)
+        deal(ca_w, ca_w_raw)
+        ca_s = tile("ca_s", [P, C], U8)
+        deal(ca_s, ca_s_raw)
+
+        def score(name, tag, words, scales, t):
+            acc = psum.tile([P, S], F32, name=name, tag=tag)
+            nc.tensor.matmul_mx(
+                acc[:],
+                lhsT=words[:, P * t : P * (t + 1)].bitcast(FP8X4),
+                lhsT_scale=scales[:, P * t : P * (t + 1)],
+                rhs=z_w[:].bitcast(FP8X4),
+                rhs_scale=z_s[:],
+                start=True,
+                stop=True,
+            )
+            return acc
+
+        b_ps = [score(f"b{t}", f"high{t}", cb_w, cb_s, t) for t in range(PACK)]
+        a_ps = [score(f"a{t}", f"low{t}", ca_w, ca_s, t) for t in range(PACK)]
+
+        tanh_b = [tile(f"tanh_b{t}", [P, S], F32) for t in range(PACK)]
+        prod = [tile(f"prod{t}", [P, S], F32) for t in range(PACK)]
+        a_sb = [tile(f"a_sb{t}", [P, S], F32) for t in range(PACK)]
+        res = [tile(f"res{i}", [P, PACK, hi - lo], F32) for i, (lo, hi) in enumerate(PIECES)]
+
+        def fetch_b(t):
+            nc.scalar.activation(half[t][:, :S], b_ps[t][:], ACT.Copy, scale=0.0625)
+            nc.scalar.activation(tanh_b[t][:], b_ps[t][:], ACT.Tanh, scale=0.0625)
+            nc.vector.tensor_tensor(prod[t][:], half[t][:].indirect(n4_t[:]), tanh_b[t][:], ALU.mult)
+
+        def fetch_a(t, i):
+            lo, hi = PIECES[i]
+            if i == 0:
+                nc.scalar.activation(a_sb[t][:], a_ps[t][:], ACT.Copy, scale=0.0625)
+            nc.vector.tensor_tensor(res[i][:, t, :], a_sb[t][:].indirect(n3_t[:, lo // 16 : hi // 16]), prod[t][:, lo:hi], ALU.subtract)
+
+        out_rows = out_0.rearrange("(p t) c -> p t c", t=PACK)
+        out_words = out_1[0].rearrange("p c t -> p (c t)").bitcast(I32)
+        o_s = tile("o_s", [P, S], U8)
+        o_bf = [tile(f"o_bf{i}", [P, hi - lo, PACK], BF16) for i, (lo, hi) in enumerate(PIECES)]
+        o_w = [tile(f"o_w{i}", [P, hi - lo], U32) for i, (lo, hi) in enumerate(PIECES)]
+
+        def round_piece(i, engine):
+            lo, hi = PIECES[i]
+            nc.sync.dma_start(out_rows[:, :, lo:hi], res[i][:])
+            dst = o_bf[i][:].rearrange("p (c j) t -> p c t j", j=4)
+            src = res[i][:].rearrange("p t (c j) -> p c t j", j=4)
+            if engine == "scalar":
+                nc.scalar.copy(dst, src)
+            else:
+                nc.vector.tensor_copy(dst, src)
+
+        def quantise_piece(i):
+            lo, hi = PIECES[i]
+            nc.vector.quantize_mx(o_w[i][:].bitcast(FP8X4), o_s[:, lo:hi], o_bf[i][:].rearrange("p c t -> p (c t)"))
+            nc.sync.dma_start(out_words[:, lo:hi], o_w[i][:].bitcast(I32))
+
+        fetch_b(0)
+        fetch_b(1)
+        fetch_a(0, 0)
+        fetch_b(2)
+        fetch_a(1, 0)
+        fetch_b(3)
+        fetch_a(2, 0)
+        fetch_a(3, 0)
+        round_piece(0, "scalar")
+        for t in range(PACK):
+            fetch_a(t, 1)
+        round_piece(1, "scalar")
+        fetch_a(0, 2)
+        fetch_a(1, 2)
+        quantise_piece(0)
+        fetch_a(2, 2)
+        fetch_a(3, 2)
+        quantise_piece(1)
+        round_piece(2, "vector")
+        quantise_piece(2)
+        for q in range(4):
+            engine = nc.scalar if q % 2 == 0 else nc.sync
+            engine.dma_start(out_2[0, 4 * q : 4 * q + 4, :].bitcast(I32), o_s[32 * q : 32 * q + 4, :].bitcast(I32))

@@ -48,13 +48,13 @@ def tile_picked_ccmpsoftbhopb_none_po_kernel(tc, x_words, x_scales, w1_words, w1
         ws_raw = tile("ws_raw", [P, H], U8)
         nc.vector.memset(ws_raw[:].bitcast(I32), 0)
 
-        offs_t = load_list("offs_t", offs)
         ww_raw = tile("ww_raw", [P, 2 * H], U8)
         nc.sync.dma_start(ww_raw[:].bitcast(I32), w1_words[0].bitcast(I32))
+        offs_t = load_list("offs_t", offs)
+        load_scale_rows([nc.sync, nc.scalar] * 2, xs, x_scales)
         xw = tile("xw", [P, T], U32)
         nc.sync.dma_start(xw[:].bitcast(I32), x_words[0].rearrange("p n t -> p (n t)").bitcast(I32))
-        load_scale_rows([nc.sync] * 4, xs, x_scales)
-        load_scale_rows([nc.sync, nc.sync, nc.gpsimd, nc.gpsimd], ws_raw, w1_scales)
+        load_scale_rows([nc.sync] * 4, ws_raw, w1_scales)
         cb_t = load_list("cb_t", cb)
         n1_t = load_list("n1_t", n1)
         n2_t = load_list("n2_t", n2)
@@ -81,7 +81,10 @@ def tile_picked_ccmpsoftbhopb_none_po_kernel(tc, x_words, x_scales, w1_words, w1
         xq_w = tile("xq_w", [P, S], U32)
         nc.vector.tensor_copy(xq_w[:], xw[:].indirect(offs_t[:]))
         ws = tile("ws", [P, H], U8)
-        deal(ws, ws_raw)
+        ws_dst = ws[:].rearrange("p (t m) -> p m t", t=PACK)
+        ws_src = ws_raw[:].rearrange("p (m t) -> p m t", t=PACK)
+        nc.vector.tensor_copy(ws_dst[:, :, 0:1], ws_src[:, :, 0:1])
+        nc.vector.tensor_copy(ws_dst[:, :, 1:PACK], ws_src[:, :, 1:PACK])
 
         y_ps = []
         for t in range(PACK):
@@ -98,12 +101,12 @@ def tile_picked_ccmpsoftbhopb_none_po_kernel(tc, x_words, x_scales, w1_words, w1
             nc.scalar.activation(half[t][:, :S], acc[:], ACT.Copy, scale=0.5)
             y_ps.append(acc)
 
-        cb_w_raw = tile("cb_w_raw", [P, C], U32)
-        nc.vector.tensor_copy(cb_w_raw[:], xw[:].indirect(cb_t[:]))
+        cb_w = tile("cb_w", [P, C], U32, tag="ws_raw")
+        nc.vector.tensor_copy(cb_w[:].rearrange("p (t m) -> p m t", t=PACK), xw[:].indirect(cb_t[:]))
 
         st = [tile(f"st{t}", [P, 2 * S], F32) for t in range(PACK)]
         diff = [tile(f"diff{t}", [P, S], F32) for t in range(PACK)]
-        z_bf = tile("z_bf", [P, S, PACK], BF16)
+        z_bf = [tile(f"z_bf{i}", [P, S // 2, PACK], BF16) for i in range(2)]
 
         def fetch_y(t):
             nc.vector.tensor_copy(st[t][:, S:], half[t][:].indirect(n1_t[:]))
@@ -111,56 +114,61 @@ def tile_picked_ccmpsoftbhopb_none_po_kernel(tc, x_words, x_scales, w1_words, w1
         def larger(t):
             nc.vector.scalar_tensor_tensor(st[t][:, :S], st[t][:, S:], 2.0, y_ps[t][:], ALU.mult, ALU.max)
 
-        def fetch_st(t):
-            nc.vector.tensor_tensor(diff[t][:], st[t][:].indirect(n2_t[:]), half[t][:, :S], ALU.subtract)
-            nc.scalar.activation(z_bf[:, :, t], diff[t][:], ACT.Copy, scale=gs_t[:, t : t + 1])
+        def fetch_st(t, lo, hi):
+            nc.vector.tensor_tensor(diff[t][:, lo:hi], st[t][:].indirect(n2_t[:, lo // 16 : hi // 16]), half[t][:, lo:hi], ALU.subtract)
+            for c in range(lo, hi, S // 2):
+                nc.scalar.activation(z_bf[c // (S // 2)][:, :, t], diff[t][:, c : c + S // 2], ACT.Copy, scale=gs_t[:, t : t + 1])
 
         fetch_y(0)
         fetch_y(1)
         larger(0)
         larger(1)
-        fetch_st(0)
+        fetch_st(0, 0, S)
         fetch_y(2)
-        fetch_st(1)
+        fetch_st(1, 0, S)
         larger(2)
         fetch_y(3)
-        fetch_st(2)
+        fetch_st(2, 0, S)
         larger(3)
-        cb_w = tile("cb_w", [P, C], U32, tag="st2")
-        deal(cb_w, cb_w_raw)
-        fetch_st(3)
-        cb_s_raw = tile("cb_s_raw", [P, C], U8, tag="st3")
+        cb_s_raw = tile("cb_s_raw", [P, C], U8, tag="st2")
         nc.vector.tensor_copy(cb_s_raw[:], xs[:].indirect(cb_t[:]))
-        cb_s = tile("cb_s", [P, C], U8)
+        fetch_st(3, 0, S // 2)
+        fetch_st(3, S // 2, S)
+        cb_s = tile("cb_s", [P, C], U8, tag="st3")
         deal(cb_s, cb_s_raw)
 
         z_w = tile("z_w", [P, S], U32)
         z_s = tile("z_s", [P, S], U8)
-        nc.vector.quantize_mx(z_w[:].bitcast(FP8X4), z_s[:], z_bf[:].rearrange("p c t -> p (c t)"))
 
-        ca_w_raw = tile("ca_w_raw", [P, C], U32, tag="z_bf")
-        nc.vector.tensor_copy(ca_w_raw[:], xw[:].indirect(ca_t[:]))
-        ca_s_raw = tile("ca_s_raw", [P, C], U8, tag="diff3")
-        nc.vector.tensor_copy(ca_s_raw[:], xs[:].indirect(ca_t[:]))
-        ca_w = tile("ca_w", [P, C], U32)
-        deal(ca_w, ca_w_raw)
+        def quantise_z(i):
+            cols = slice(i * (S // 2), (i + 1) * (S // 2))
+            nc.vector.quantize_mx(z_w[:, cols].bitcast(FP8X4), z_s[:, cols], z_bf[i][:].rearrange("p c t -> p (c t)"))
+
+        quantise_z(0)
+        ca_s_raw = tile("ca_s_raw", [P, C], U8, tag="z_bf0")
+        nc.vector.tensor_copy(ca_s_raw[:, : C // 2], xs[:].indirect(ca_t[:, : C // 32]))
+        quantise_z(1)
+        ca_w = tile("ca_w", [P, C], U32, tag="z_bf1")
+        nc.vector.tensor_copy(ca_s_raw[:, C // 2 :], xs[:].indirect(ca_t[:, C // 32 :]))
+        nc.vector.tensor_copy(ca_w[:].rearrange("p (t m) -> p m t", t=PACK), xw[:].indirect(ca_t[:]))
         ca_s = tile("ca_s", [P, C], U8)
         deal(ca_s, ca_s_raw)
 
-        def score(name, tag, words, scales, t):
+        def score(name, tag, words, scales, t, width=S):
             acc = psum.tile([P, S], F32, name=name, tag=tag)
-            nc.tensor.matmul_mx(
-                acc[:],
-                lhsT=words[:, P * t : P * (t + 1)].bitcast(FP8X4),
-                lhsT_scale=scales[:, P * t : P * (t + 1)],
-                rhs=z_w[:].bitcast(FP8X4),
-                rhs_scale=z_s[:],
-                start=True,
-                stop=True,
-            )
+            for c in range(0, S, width):
+                nc.tensor.matmul_mx(
+                    acc[:, c : c + width],
+                    lhsT=words[:, P * t : P * (t + 1)].bitcast(FP8X4),
+                    lhsT_scale=scales[:, P * t : P * (t + 1)],
+                    rhs=z_w[:, c : c + width].bitcast(FP8X4),
+                    rhs_scale=z_s[:, c : c + width],
+                    start=True,
+                    stop=True,
+                )
             return acc
 
-        b_ps = [score(f"b{t}", f"high{t}", cb_w, cb_s, t) for t in range(PACK)]
+        b_ps = [score(f"b{t}", f"high{t}", cb_w, cb_s, t, S // 2 if t == 0 else S) for t in range(PACK)]
         a_ps = [score(f"a{t}", f"low{t}", ca_w, ca_s, t) for t in range(PACK)]
 
         tanh_b = [tile(f"tanh_b{t}", [P, S], F32) for t in range(PACK)]

@@ -18,6 +18,7 @@ ACT = mybir.ActivationFunctionType
 
 P = 128
 PACK = 4
+HALF = 256
 PIECES = ((0, 256), (256, 384), (384, 512))
 
 
@@ -41,7 +42,7 @@ def tile_picked_ccmpsoftbhopb_none_po_kernel(tc, x_words, x_scales, w1_words, w1
                 engine.dma_start(dst[32 * q : 32 * q + 4, :].bitcast(I32), src[0, 4 * q : 4 * q + 4, :].bitcast(I32))
 
         def deal(dst, src):
-            nc.vector.tensor_copy(dst[:].rearrange("p (t m) -> p m t", t=PACK), src[:].rearrange("p (m t) -> p m t", t=PACK))
+            nc.vector.tensor_copy(dst[:].rearrange("p (t m) -> p t m", t=PACK), src[:].rearrange("p (m t) -> p t m", t=PACK))
 
         xs = tile("xs", [P, T], U8)
         nc.vector.memset(xs[:].bitcast(I32), 0)
@@ -51,11 +52,11 @@ def tile_picked_ccmpsoftbhopb_none_po_kernel(tc, x_words, x_scales, w1_words, w1
         ww_raw = tile("ww_raw", [P, 2 * H], U8)
         nc.sync.dma_start(ww_raw[:].bitcast(I32), w1_words[0].bitcast(I32))
         offs_t = load_list("offs_t", offs)
+        cb_t = load_list("cb_t", cb)
         load_scale_rows([nc.sync, nc.scalar] * 2, xs, x_scales)
         xw = tile("xw", [P, T], U32)
         nc.sync.dma_start(xw[:].bitcast(I32), x_words[0].rearrange("p n t -> p (n t)").bitcast(I32))
         load_scale_rows([nc.sync] * 4, ws_raw, w1_scales)
-        cb_t = load_list("cb_t", cb)
         n1_t = load_list("n1_t", n1)
         n2_t = load_list("n2_t", n2)
         gs_t = tile("gs_t", [P, PACK], F32)
@@ -73,18 +74,20 @@ def tile_picked_ccmpsoftbhopb_none_po_kernel(tc, x_words, x_scales, w1_words, w1
 
         ww = tile("ww", [P, 2 * H], U8)
         nc.vector.tensor_copy(
-            ww[:].rearrange("p (t m b) -> p m t b", t=PACK, b=2),
-            ww_raw[:].rearrange("p (m t b) -> p m t b", t=PACK, b=2),
+            ww[:].rearrange("p (t m b) -> p t m b", t=PACK, b=2),
+            ww_raw[:].rearrange("p (m t b) -> p t m b", t=PACK, b=2),
         )
         xq_s = tile("xq_s", [P, S], U8)
         nc.vector.tensor_copy(xq_s[:], xs[:].indirect(offs_t[:]))
+        cb_s_raw = tile("cb_s_raw", [P, C], U8)
+        nc.vector.tensor_copy(cb_s_raw[:], xs[:].indirect(cb_t[:]))
         xq_w = tile("xq_w", [P, S], U32)
         nc.vector.tensor_copy(xq_w[:], xw[:].indirect(offs_t[:]))
         ws = tile("ws", [P, H], U8)
-        ws_dst = ws[:].rearrange("p (t m) -> p m t", t=PACK)
-        ws_src = ws_raw[:].rearrange("p (m t) -> p m t", t=PACK)
-        nc.vector.tensor_copy(ws_dst[:, :, 0:1], ws_src[:, :, 0:1])
-        nc.vector.tensor_copy(ws_dst[:, :, 1:PACK], ws_src[:, :, 1:PACK])
+        ws_dst = ws[:].rearrange("p (t m) -> p t m", t=PACK)
+        ws_src = ws_raw[:].rearrange("p (m t) -> p t m", t=PACK)
+        nc.vector.tensor_copy(ws_dst[:, 0:2, :], ws_src[:, 0:2, :])
+        nc.vector.tensor_copy(ws_dst[:, 2:PACK, :], ws_src[:, 2:PACK, :])
 
         y_ps = []
         for t in range(PACK):
@@ -101,7 +104,9 @@ def tile_picked_ccmpsoftbhopb_none_po_kernel(tc, x_words, x_scales, w1_words, w1
             nc.scalar.activation(half[t][:, :S], acc[:], ACT.Copy, scale=0.5)
             y_ps.append(acc)
 
-        cb_w = tile("cb_w", [P, C], U32, tag="ws_raw")
+        cb_s = tile("cb_s", [P, C], U8, tag="ws_raw")
+        deal(cb_s, cb_s_raw)
+        cb_w = tile("cb_w", [P, C], U32, tag="cb_s_raw")
         nc.vector.tensor_copy(cb_w[:].rearrange("p (t m) -> p m t", t=PACK), xw[:].indirect(cb_t[:]))
 
         st = [tile(f"st{t}", [P, 2 * S], F32) for t in range(PACK)]
@@ -130,12 +135,11 @@ def tile_picked_ccmpsoftbhopb_none_po_kernel(tc, x_words, x_scales, w1_words, w1
         fetch_y(3)
         fetch_st(2, 0, S)
         larger(3)
-        cb_s_raw = tile("cb_s_raw", [P, C], U8, tag="st2")
-        nc.vector.tensor_copy(cb_s_raw[:], xs[:].indirect(cb_t[:]))
+        ca_s_raw = tile("ca_s_raw", [P, C], U8, tag="st2")
+        nc.vector.tensor_copy(ca_s_raw[:, : C // 2], xs[:].indirect(ca_t[:, : C // 32]))
         fetch_st(3, 0, S // 2)
         fetch_st(3, S // 2, S)
-        cb_s = tile("cb_s", [P, C], U8, tag="st3")
-        deal(cb_s, cb_s_raw)
+        nc.vector.tensor_copy(ca_s_raw[:, C // 2 :], xs[:].indirect(ca_t[:, C // 32 :]))
 
         z_w = tile("z_w", [P, S], U32)
         z_s = tile("z_s", [P, S], U8)
@@ -145,63 +149,58 @@ def tile_picked_ccmpsoftbhopb_none_po_kernel(tc, x_words, x_scales, w1_words, w1
             nc.vector.quantize_mx(z_w[:, cols].bitcast(FP8X4), z_s[:, cols], z_bf[i][:].rearrange("p c t -> p (c t)"))
 
         quantise_z(0)
-        ca_s_raw = tile("ca_s_raw", [P, C], U8, tag="z_bf0")
-        nc.vector.tensor_copy(ca_s_raw[:, : C // 2], xs[:].indirect(ca_t[:, : C // 32]))
-        quantise_z(1)
-        ca_w = tile("ca_w", [P, C], U32, tag="z_bf1")
-        nc.vector.tensor_copy(ca_s_raw[:, C // 2 :], xs[:].indirect(ca_t[:, C // 32 :]))
-        nc.vector.tensor_copy(ca_w[:].rearrange("p (t m) -> p m t", t=PACK), xw[:].indirect(ca_t[:]))
         ca_s = tile("ca_s", [P, C], U8)
         deal(ca_s, ca_s_raw)
+        quantise_z(1)
+        ca_w = tile("ca_w", [P, C], U32, tag="z_bf1")
+        nc.vector.tensor_copy(ca_w[:].rearrange("p (t m) -> p m t", t=PACK), xw[:].indirect(ca_t[:]))
 
-        def score(name, tag, words, scales, t, width=S):
-            acc = psum.tile([P, S], F32, name=name, tag=tag)
-            for c in range(0, S, width):
-                nc.tensor.matmul_mx(
-                    acc[:, c : c + width],
-                    lhsT=words[:, P * t : P * (t + 1)].bitcast(FP8X4),
-                    lhsT_scale=scales[:, P * t : P * (t + 1)],
-                    rhs=z_w[:, c : c + width].bitcast(FP8X4),
-                    rhs_scale=z_s[:, c : c + width],
-                    start=True,
-                    stop=True,
-                )
-            return acc
+        def score(name, tag, words, scales, t, lo, hi):
+            acc = psum.tile([P, hi - lo], F32, name=name, tag=tag)
+            nc.tensor.matmul_mx(
+                acc[:],
+                lhsT=words[:, P * t : P * (t + 1)].bitcast(FP8X4),
+                lhsT_scale=scales[:, P * t : P * (t + 1)],
+                rhs=z_w[:, lo:hi].bitcast(FP8X4),
+                rhs_scale=z_s[:, lo:hi],
+                start=True,
+                stop=True,
+            )
+            return acc, lo, hi
 
-        b_ps = [score(f"b{t}", f"high{t}", cb_w, cb_s, t, S // 2 if t == 0 else S) for t in range(PACK)]
-        a_ps = [score(f"a{t}", f"low{t}", ca_w, ca_s, t) for t in range(PACK)]
+        b_ps = [[score("b0a", "low3", cb_w, cb_s, 0, 0, HALF), score("b0b", "high0", cb_w, cb_s, 0, HALF, S)]]
+        b_ps += [[score(f"b{t}", f"high{t}", cb_w, cb_s, t, 0, S)] for t in range(1, PACK)]
+        a_ps = [score(f"a{t}", f"low{t}", ca_w, ca_s, t, 0, S)[0] for t in range(PACK)]
 
         tanh_b = [tile(f"tanh_b{t}", [P, S], F32) for t in range(PACK)]
         prod = [tile(f"prod{t}", [P, S], F32) for t in range(PACK)]
         a_sb = [tile(f"a_sb{t}", [P, S], F32) for t in range(PACK)]
-        res = [tile(f"res{i}", [P, PACK, hi - lo], F32) for i, (lo, hi) in enumerate(PIECES)]
+        res = [tile(f"res{i}", [P, PACK, HALF], F32) for i in range(2)]
 
         def fetch_b(t):
-            nc.scalar.activation(half[t][:, :S], b_ps[t][:], ACT.Copy, scale=0.0625)
-            nc.scalar.activation(tanh_b[t][:], b_ps[t][:], ACT.Tanh, scale=0.0625)
+            for acc, lo, hi in b_ps[t]:
+                nc.scalar.activation(half[t][:, lo:hi], acc[:], ACT.Copy, scale=0.0625)
+                nc.scalar.activation(tanh_b[t][:, lo:hi], acc[:], ACT.Tanh, scale=0.0625)
             nc.vector.tensor_tensor(prod[t][:], half[t][:].indirect(n4_t[:]), tanh_b[t][:], ALU.mult)
 
-        def fetch_a(t, i):
-            lo, hi = PIECES[i]
-            if i == 0:
-                nc.scalar.activation(a_sb[t][:], a_ps[t][:], ACT.Copy, scale=0.0625)
-            nc.vector.tensor_tensor(res[i][:, t, :], a_sb[t][:].indirect(n3_t[:, lo // 16 : hi // 16]), prod[t][:, lo:hi], ALU.subtract)
-
         out_rows = out_0.rearrange("(p t) c -> p t c", t=PACK)
+
+        def fetch_a(t, lo, hi):
+            if lo == 0:
+                nc.scalar.activation(a_sb[t][:], a_ps[t][:], ACT.Copy, scale=0.0625)
+            dst = res[lo // HALF][:, t, lo % HALF : lo % HALF + hi - lo]
+            nc.vector.tensor_tensor(dst, a_sb[t][:].indirect(n3_t[:, lo // 16 : hi // 16]), prod[t][:, lo:hi], ALU.subtract)
+
         out_words = out_1[0].rearrange("p c t -> p (c t)").bitcast(I32)
         o_s = tile("o_s", [P, S], U8)
         o_bf = [tile(f"o_bf{i}", [P, hi - lo, PACK], BF16) for i, (lo, hi) in enumerate(PIECES)]
         o_w = [tile(f"o_w{i}", [P, hi - lo], U32) for i, (lo, hi) in enumerate(PIECES)]
 
-        def round_piece(i, engine):
+        def round_piece(i, copy):
             lo, hi = PIECES[i]
-            nc.sync.dma_start(out_rows[:, :, lo:hi], res[i][:])
             dst = o_bf[i][:].rearrange("p (c j) t -> p c t j", j=4)
-            src = res[i][:].rearrange("p t (c j) -> p c t j", j=4)
-            if engine == "scalar":
-                nc.scalar.copy(dst, src)
-            else:
-                nc.vector.tensor_copy(dst, src)
+            src = res[lo // HALF][:, :, lo % HALF : lo % HALF + hi - lo].rearrange("p t (c j) -> p c t j", j=4)
+            copy(dst, src)
 
         def quantise_piece(i):
             lo, hi = PIECES[i]
@@ -210,23 +209,24 @@ def tile_picked_ccmpsoftbhopb_none_po_kernel(tc, x_words, x_scales, w1_words, w1
 
         fetch_b(0)
         fetch_b(1)
-        fetch_a(0, 0)
+        fetch_a(0, 0, HALF)
         fetch_b(2)
-        fetch_a(1, 0)
+        fetch_a(1, 0, HALF)
         fetch_b(3)
-        fetch_a(2, 0)
-        fetch_a(3, 0)
-        round_piece(0, "scalar")
-        for t in range(PACK):
-            fetch_a(t, 1)
-        round_piece(1, "scalar")
-        fetch_a(0, 2)
-        fetch_a(1, 2)
+        fetch_a(2, 0, HALF)
+        fetch_a(3, 0, HALF)
+        nc.sync.dma_start(out_rows[:, :, :HALF], res[0][:])
+        round_piece(0, nc.scalar.copy)
+        for t in range(PACK - 1):
+            fetch_a(t, HALF, S)
+        nc.sync.dma_start(out_rows[:, : PACK - 1, HALF:], res[1][:, : PACK - 1, :])
         quantise_piece(0)
-        fetch_a(2, 2)
-        fetch_a(3, 2)
+        fetch_a(3, *PIECES[1])
+        round_piece(1, nc.scalar.copy)
+        fetch_a(3, *PIECES[2])
+        nc.sync.dma_start(out_rows[:, PACK - 1, HALF:], res[1][:, PACK - 1, :])
+        round_piece(2, nc.vector.tensor_copy)
         quantise_piece(1)
-        round_piece(2, "vector")
         quantise_piece(2)
         for q in range(4):
             engine = nc.scalar if q % 2 == 0 else nc.sync

@@ -52,8 +52,8 @@ def tile_picked_ccmpsoftbhopb_none_po_kernel(tc, x_words, x_scales, w1_words, w1
         ww_raw = tile("ww_raw", [P, 2 * H], U8)
         nc.sync.dma_start(ww_raw[:].bitcast(I32), w1_words[0].bitcast(I32))
         offs_t = load_list("offs_t", offs)
-        cb_t = load_list("cb_t", cb)
         load_scale_rows([nc.sync, nc.scalar] * 2, xs, x_scales)
+        cb_t = load_list("cb_t", cb)
         xw = tile("xw", [P, T], U32)
         nc.sync.dma_start(xw[:].bitcast(I32), x_words[0].rearrange("p n t -> p (n t)").bitcast(I32))
         load_scale_rows([nc.sync] * 4, ws_raw, w1_scales)
@@ -66,11 +66,10 @@ def tile_picked_ccmpsoftbhopb_none_po_kernel(tc, x_words, x_scales, w1_words, w1
         n3_t = load_list("n3_t", n3)
 
         half = [tile(f"half{t}", [P, 2 * S], F32) for t in range(PACK)]
+        zero = tile("zero", [P, 1], F32)
+        nc.vector.memset(zero[:], 0.0)
         for t in range(PACK):
-            nc.vector.memset(half[t][:, S:], 0.0)
-
-        warm = tile("warm", [P, 1], F32)
-        nc.scalar.activation(warm[:], half[0][:, S : S + 1], ACT.Tanh)
+            nc.scalar.activation(half[t][:, S:], zero[:].to_broadcast([P, S]), ACT.Tanh)
 
         ww = tile("ww", [P, 2 * H], U8)
         nc.vector.tensor_copy(
@@ -194,7 +193,7 @@ def tile_picked_ccmpsoftbhopb_none_po_kernel(tc, x_words, x_scales, w1_words, w1
         out_words = out_1[0].rearrange("p c t -> p (c t)").bitcast(I32)
         o_s = tile("o_s", [P, S], U8)
         o_bf = [tile(f"o_bf{i}", [P, hi - lo, PACK], BF16) for i, (lo, hi) in enumerate(PIECES)]
-        o_w = [tile(f"o_w{i}", [P, hi - lo], U32) for i, (lo, hi) in enumerate(PIECES)]
+        o_w = [tile(f"o_w{i}", [P, HALF], U32) for i in range(2)]
 
         def round_piece(i, copy):
             lo, hi = PIECES[i]
@@ -204,8 +203,10 @@ def tile_picked_ccmpsoftbhopb_none_po_kernel(tc, x_words, x_scales, w1_words, w1
 
         def quantise_piece(i):
             lo, hi = PIECES[i]
-            nc.vector.quantize_mx(o_w[i][:].bitcast(FP8X4), o_s[:, lo:hi], o_bf[i][:].rearrange("p c t -> p (c t)"))
-            nc.sync.dma_start(out_words[:, lo:hi], o_w[i][:].bitcast(I32))
+            words = o_w[lo // HALF]
+            nc.vector.quantize_mx(words[:, lo % HALF : lo % HALF + hi - lo].bitcast(FP8X4), o_s[:, lo:hi], o_bf[i][:].rearrange("p c t -> p (c t)"))
+            if hi % HALF == 0:
+                nc.sync.dma_start(out_words[:, hi - HALF : hi], words[:].bitcast(I32))
 
         fetch_b(0)
         fetch_b(1)

from contextlib import ExitStack

import concourse.mybir as mybir

K, T, S, H, C = 512, 2048, 512, 512, 512
FLOPS = 3 * 2 * 512 * 512 * 512

F32 = mybir.dt.float32
BF16 = mybir.dt.bfloat16
I32 = mybir.dt.int32
U32 = mybir.dt.uint32
U16 = mybir.dt.uint16
U8 = mybir.dt.uint8
FP8X4 = mybir.dt.float8_e4m3fn_x4
FP4X4 = mybir.dt.float4_e2m1fn_x4
ALU = mybir.AluOpType
ACT = mybir.ActivationFunctionType

P = 128
PACK = 4
HALF = 256
PIECES = ((0, 256), (256, 384), (384, 512))


def tile_picked_ccmpsoftbhopb_none_po_kernel(tc, x_words, x_scales, w1_words, w1_scales, gs, offs, n1, n2, ca, cb, n3, n4, out_0, out_1, out_2):
    nc = tc.nc
    with ExitStack() as ctx:
        lists = ctx.enter_context(tc.tile_pool(name="lists", bufs=1))
        sb = ctx.enter_context(tc.tile_pool(name="sb", bufs=1))
        psum = ctx.enter_context(tc.psum_pool(name="psum", bufs=1))

        def tile(name, shape, dtype, tag=None):
            return sb.tile(shape, dtype, name=name, tag=tag or name, align_bytes=64)

        def load_list(name, src):
            dst = lists.tile([P, S // 16], U16, name=name)
            nc.sync.dma_start(dst[:], src)
            return dst

        def load_scale_rows(engines, dst, src):
            for q, engine in enumerate(engines):
                engine.dma_start(dst[32 * q : 32 * q + 4, :].bitcast(I32), src[0, 4 * q : 4 * q + 4, :].bitcast(I32))

        def deal(dst, src):
            nc.vector.tensor_copy(dst[:].rearrange("p (t m) -> p t m", t=PACK), src[:].rearrange("p (m t) -> p t m", t=PACK))

        xs = tile("xs", [P, T], U8)
        nc.vector.memset(xs[:].bitcast(I32), 0)
        ws_raw = tile("ws_raw", [P, H], U8)
        nc.vector.memset(ws_raw[:].bitcast(I32), 0)

        ww_raw = tile("ww_raw", [P, 2 * H], U8)
        nc.sync.dma_start(ww_raw[:].bitcast(I32), w1_words[0].bitcast(I32))
        offs_t = load_list("offs_t", offs)
        load_scale_rows([nc.sync, nc.scalar] * 2, xs, x_scales)
        cb_t = load_list("cb_t", cb)
        xw = tile("xw", [P, T], U32)
        nc.sync.dma_start(xw[:].bitcast(I32), x_words[0].rearrange("p n t -> p (n t)").bitcast(I32))
        load_scale_rows([nc.sync] * 4, ws_raw, w1_scales)
        n1_t = load_list("n1_t", n1)
        n2_t = load_list("n2_t", n2)
        gs_t = tile("gs_t", [P, PACK], F32)
        nc.sync.dma_start(gs_t[:], gs.rearrange("(p t) o -> p (t o)", t=PACK))
        ca_t = load_list("ca_t", ca)
        n4_t = load_list("n4_t", n4)
        n3_t = load_list("n3_t", n3)

        half = [tile(f"half{t}", [P, 2 * S], F32) for t in range(PACK)]
        zero = tile("zero", [P, 1], F32)
        nc.vector.memset(zero[:], 0.0)
        for t in range(PACK):
            nc.scalar.activation(half[t][:, S:], zero[:].to_broadcast([P, S]), ACT.Tanh)

        ww = tile("ww", [P, 2 * H], U8)
        nc.vector.tensor_copy(
            ww[:].rearrange("p (t m b) -> p t m b", t=PACK, b=2),
            ww_raw[:].rearrange("p (m t b) -> p t m b", t=PACK, b=2),
        )
        xq_s = tile("xq_s", [P, S], U8)
        nc.vector.tensor_copy(xq_s[:], xs[:].indirect(offs_t[:]))
        cb_s_raw = tile("cb_s_raw", [P, C], U8)
        nc.vector.tensor_copy(cb_s_raw[:], xs[:].indirect(cb_t[:]))
        xq_w = tile("xq_w", [P, S], U32)
        nc.vector.tensor_copy(xq_w[:], xw[:].indirect(offs_t[:]))
        ws = tile("ws", [P, H], U8)
        ws_dst = ws[:].rearrange("p (t m) -> p t m", t=PACK)
        ws_src = ws_raw[:].rearrange("p (m t) -> p t m", t=PACK)
        nc.vector.tensor_copy(ws_dst[:, 0:2, :], ws_src[:, 0:2, :])
        nc.vector.tensor_copy(ws_dst[:, 2:PACK, :], ws_src[:, 2:PACK, :])

        y_ps = []
        for t in range(PACK):
            acc = psum.tile([P, S], F32, name=f"y{t}", tag=f"low{t}")
            nc.tensor.matmul_mx(
                acc[:],
                lhsT=ww[:, 2 * P * t : 2 * P * (t + 1)].bitcast(FP4X4),
                lhsT_scale=ws[:, P * t : P * (t + 1)],
                rhs=xq_w[:].bitcast(FP8X4),
                rhs_scale=xq_s[:],
                start=True,
                stop=True,
            )
            nc.scalar.activation(half[t][:, :S], acc[:], ACT.Copy, scale=0.5)
            y_ps.append(acc)

        cb_s = tile("cb_s", [P, C], U8, tag="ws_raw")
        deal(cb_s, cb_s_raw)
        cb_w = tile("cb_w", [P, C], U32, tag="cb_s_raw")
        nc.vector.tensor_copy(cb_w[:].rearrange("p (t m) -> p m t", t=PACK), xw[:].indirect(cb_t[:]))

        st = [tile(f"st{t}", [P, 2 * S], F32) for t in range(PACK)]
        diff = [tile(f"diff{t}", [P, S], F32) for t in range(PACK)]
        z_bf = [tile(f"z_bf{i}", [P, S // 2, PACK], BF16) for i in range(2)]

        def fetch_y(t):
            nc.vector.tensor_copy(st[t][:, S:], half[t][:].indirect(n1_t[:]))

        def larger(t):
            nc.vector.scalar_tensor_tensor(st[t][:, :S], st[t][:, S:], 2.0, y_ps[t][:], ALU.mult, ALU.max)

        def fetch_st(t, lo, hi):
            nc.vector.tensor_tensor(diff[t][:, lo:hi], st[t][:].indirect(n2_t[:, lo // 16 : hi // 16]), half[t][:, lo:hi], ALU.subtract)
            for c in range(lo, hi, S // 2):
                nc.scalar.activation(z_bf[c // (S // 2)][:, :, t], diff[t][:, c : c + S // 2], ACT.Copy, scale=gs_t[:, t : t + 1])

        fetch_y(0)
        fetch_y(1)
        larger(0)
        larger(1)
        fetch_st(0, 0, S)
        fetch_y(2)
        fetch_st(1, 0, S)
        larger(2)
        fetch_y(3)
        fetch_st(2, 0, S)
        larger(3)
        ca_s_raw = tile("ca_s_raw", [P, C], U8, tag="st2")
        nc.vector.tensor_copy(ca_s_raw[:, : C // 2], xs[:].indirect(ca_t[:, : C // 32]))
        fetch_st(3, 0, S // 2)
        fetch_st(3, S // 2, S)
        nc.vector.tensor_copy(ca_s_raw[:, C // 2 :], xs[:].indirect(ca_t[:, C // 32 :]))

        z_w = tile("z_w", [P, S], U32)
        z_s = tile("z_s", [P, S], U8)

        def quantise_z(i):
            cols = slice(i * (S // 2), (i + 1) * (S // 2))
            nc.vector.quantize_mx(z_w[:, cols].bitcast(FP8X4), z_s[:, cols], z_bf[i][:].rearrange("p c t -> p (c t)"))

        quantise_z(0)
        ca_s = tile("ca_s", [P, C], U8)
        deal(ca_s, ca_s_raw)
        quantise_z(1)
        ca_w = tile("ca_w", [P, C], U32, tag="z_bf1")
        nc.vector.tensor_copy(ca_w[:].rearrange("p (t m) -> p m t", t=PACK), xw[:].indirect(ca_t[:]))

        def score(name, tag, words, scales, t, lo, hi):
            acc = psum.tile([P, hi - lo], F32, name=name, tag=tag)
            nc.tensor.matmul_mx(
                acc[:],
                lhsT=words[:, P * t : P * (t + 1)].bitcast(FP8X4),
                lhsT_scale=scales[:, P * t : P * (t + 1)],
                rhs=z_w[:, lo:hi].bitcast(FP8X4),
                rhs_scale=z_s[:, lo:hi],
                start=True,
                stop=True,
            )
            return acc, lo, hi

        b_ps = [[score("b0a", "low3", cb_w, cb_s, 0, 0, HALF), score("b0b", "high0", cb_w, cb_s, 0, HALF, S)]]
        b_ps += [[score(f"b{t}", f"high{t}", cb_w, cb_s, t, 0, S)] for t in range(1, PACK)]
        a_ps = [score(f"a{t}", f"low{t}", ca_w, ca_s, t, 0, S)[0] for t in range(PACK)]

        tanh_b = [tile(f"tanh_b{t}", [P, S], F32) for t in range(PACK)]
        prod = [tile(f"prod{t}", [P, S], F32) for t in range(PACK)]
        a_sb = [tile(f"a_sb{t}", [P, S], F32) for t in range(PACK)]
        res = [tile(f"res{i}", [P, PACK, HALF], F32) for i in range(2)]

        def fetch_b(t):
            for acc, lo, hi in b_ps[t]:
                nc.scalar.activation(half[t][:, lo:hi], acc[:], ACT.Copy, scale=0.0625)
                nc.scalar.activation(tanh_b[t][:, lo:hi], acc[:], ACT.Tanh, scale=0.0625)
            nc.vector.tensor_tensor(prod[t][:], half[t][:].indirect(n4_t[:]), tanh_b[t][:], ALU.mult)

        out_rows = out_0.rearrange("(p t) c -> p t c", t=PACK)

        def fetch_a(t, lo, hi):
            if lo == 0:
                nc.scalar.activation(a_sb[t][:], a_ps[t][:], ACT.Copy, scale=0.0625)
            dst = res[lo // HALF][:, t, lo % HALF : lo % HALF + hi - lo]
            nc.vector.tensor_tensor(dst, a_sb[t][:].indirect(n3_t[:, lo // 16 : hi // 16]), prod[t][:, lo:hi], ALU.subtract)

        out_words = out_1[0].rearrange("p c t -> p (c t)").bitcast(I32)
        o_s = tile("o_s", [P, S], U8)
        o_bf = [tile(f"o_bf{i}", [P, hi - lo, PACK], BF16) for i, (lo, hi) in enumerate(PIECES)]
        o_w = [tile(f"o_w{i}", [P, HALF], U32) for i in range(2)]

        def round_piece(i, copy):
            lo, hi = PIECES[i]
            dst = o_bf[i][:].rearrange("p (c j) t -> p c t j", j=4)
            src = res[lo // HALF][:, :, lo % HALF : lo % HALF + hi - lo].rearrange("p t (c j) -> p c t j", j=4)
            copy(dst, src)

        def quantise_piece(i):
            lo, hi = PIECES[i]
            words = o_w[lo // HALF]
            nc.vector.quantize_mx(words[:, lo % HALF : lo % HALF + hi - lo].bitcast(FP8X4), o_s[:, lo:hi], o_bf[i][:].rearrange("p c t -> p (c t)"))
            if hi % HALF == 0:
                nc.sync.dma_start(out_words[:, hi - HALF : hi], words[:].bitcast(I32))

        fetch_b(0)
        fetch_b(1)
        fetch_a(0, 0, HALF)
        fetch_b(2)
        fetch_a(1, 0, HALF)
        fetch_b(3)
        fetch_a(2, 0, HALF)
        fetch_a(3, 0, HALF)
        nc.sync.dma_start(out_rows[:, :, :HALF], res[0][:])
        round_piece(0, nc.scalar.copy)
        for t in range(PACK - 1):
            fetch_a(t, HALF, S)
        nc.sync.dma_start(out_rows[:, : PACK - 1, HALF:], res[1][:, : PACK - 1, :])
        quantise_piece(0)
        fetch_a(3, *PIECES[1])
        round_piece(1, nc.scalar.copy)
        fetch_a(3, *PIECES[2])
        nc.sync.dma_start(out_rows[:, PACK - 1, HALF:], res[1][:, PACK - 1, :])
        round_piece(2, nc.vector.tensor_copy)
        quantise_piece(1)
        quantise_piece(2)
        for q in range(4):
            engine = nc.scalar if q % 2 == 0 else nc.sync
            engine.dma_start(out_2[0, 4 * q : 4 * q + 4, :].bitcast(I32), o_s[32 * q : 32 * q + 4, :].bitcast(I32))
